import numpy as np
import ml_dtypes


def mxq(x, axis, fmt="e4m3"):
    dtype, down = {"e4m3": (ml_dtypes.float8_e4m3fn, 7), "e5m2": (ml_dtypes.float8_e5m2, 14)}[fmt]
    v = np.moveaxis(np.asarray(x, np.float32).astype(ml_dtypes.bfloat16).astype(np.float64), axis, -1)
    blocks = v.reshape(v.shape[:-1] + (-1, 32))
    amax = np.abs(blocks).max(-1, keepdims=True)
    byte = np.maximum(np.where(amax > 0, np.frexp(amax)[1] - 1 + 127, 0) - down, 1)
    scale = np.exp2(byte - 127.0)
    codes = (blocks / scale).astype(np.float32).astype(dtype).astype(np.float64)
    return np.moveaxis((codes * scale).reshape(v.shape), -1, axis)


WIDE = False


def mx_kscale(k):
    if not WIDE:
        return np.ones(k)
    levels = np.array([10, -10, 5, -5, 0])
    if k % 512:
        return np.exp2(np.random.permutation(np.resize(levels, k // 32))).repeat(32)
    a = np.empty((k // 512, 16))
    for p in range(k // 512):
        a[p, :8] = np.random.permutation(np.resize(levels, 8))
        for g in range(8):
            far = levels[np.abs(levels - a[p, g]) >= 10]
            a[p, g + 8] = far[np.random.randint(len(far))]
    return np.exp2(a.ravel()).repeat(32)


def f64(x):
    return np.asarray(x).astype(np.float64)


def striped(idx):
    return np.tile(np.asarray(idx).reshape(-1, 16).T, (8, 1)).astype(np.uint16)


def unstriped(offs):
    return offs[:16].T.reshape(-1).astype(np.int64)


E2M1 = np.array([0.0, 0.5, 1.0, 1.5, 2.0, 3.0, 4.0, 6.0, -0.0, -0.5, -1.0, -1.5, -2.0, -3.0, -4.0, -6.0])


def pack_weight(w, fmt):
    k, n = w.shape
    w = f64(np.asarray(w, np.float32).astype(ml_dtypes.bfloat16)).reshape(k // 32, 32, n)
    amax = np.abs(w).max(1)
    if fmt == "e4m3":
        byte = np.frexp(amax)[1] - 1 + 127 - 7
    else:
        mant, ex = np.frexp(amax / 6.0)
        byte = np.where(mant > 0.5, ex, ex - 1) + 127
    byte = np.clip(np.where(amax > 0, byte, 1), 1, 254)
    scaled = (w * np.exp2(127.0 - byte)[:, None, :]).reshape(k, n).astype(np.float32)
    by_word = np.ascontiguousarray(scaled.reshape(k // 512, 128, 4, n).transpose(0, 1, 3, 2))
    if fmt == "e4m3":
        words = by_word.astype(ml_dtypes.float8_e4m3fn).view(np.uint8)
    else:
        c = by_word.astype(ml_dtypes.float4_e2m1fn).view(np.uint8) & 0xF
        words = (c[..., 0::2] | (c[..., 1::2] << 4)).reshape(k // 512, 128, 2 * n)
    return np.ascontiguousarray(words), np.ascontiguousarray(byte.astype(np.uint8).reshape(k // 512, 16, n))


def unpack_weight(words, scales, fmt):
    g, _, n = scales.shape
    words = np.ascontiguousarray(words).reshape(g, 128, n, -1)
    if fmt == "e4m3":
        vals = words.view(ml_dtypes.float8_e4m3fn).astype(np.float64)
    else:
        nib = np.empty((g, 128, n, 4), np.uint8)
        nib[..., 0::2] = words & 0xF
        nib[..., 1::2] = words >> 4
        vals = E2M1[nib]
    vals = vals * np.repeat(np.exp2(scales.astype(np.float64) - 127.0), 8, axis=1)[..., None]
    return vals.transpose(0, 1, 3, 2).reshape(g * 512, n)


D, E, T, I, Q, U = 512, 512, 1024, 256, 512, 1024


def setup_inputs():
    n = np.random.standard_normal
    idx = np.random.permutation(T)[:I]
    idx4 = np.random.permutation(U)[:I]
    fd = mx_kscale(D)
    fe = mx_kscale(E)
    fq = mx_kscale(Q)
    keysp = pack_weight(n((D, T)) / fd[:, None], "e2m1")
    valsp = pack_weight(n((E, T)) / fe[:, None], "e2m1")
    return {
        "query": (n((D, Q)) * 0.6 / np.sqrt(D) * fd[:, None]).astype(np.float32),
        "keys_words": keysp[0],
        "keys_scales": keysp[1],
        "age": np.tile(np.random.uniform(0.0, 2.0, T), (128, 1)).astype(np.float32),
        "rate": (np.random.uniform(0.3, 1.2, (Q, 1))).astype(np.float32),
        "reserve": (np.random.uniform(20.0, 100.0, (Q, 1))).astype(np.float32),
        "gout": (n((E, Q)) * 1 / np.sqrt(E) * fe[:, None]).astype(np.float32),
        "vals_words": valsp[0],
        "vals_scales": valsp[1],
        "size": (np.random.uniform(0.5, 2.0, (1, I))).astype(np.float32),
        "qs": (np.random.uniform(100.0, 400.0, (Q, 1)) * fq[:, None]).astype(np.float32),
        "qrows": (n((Q, D)) / fq[:, None]).astype(np.float32),
        "old": (n((D, U)) * 4.0).astype(np.float32),
        "fade": (np.random.uniform(0.5, 1.0, (1, U))).astype(np.float32),
        "offs": striped(idx),
        "offs4": striped(idx4),
    }


def reference(query, keys_words, keys_scales, age, rate, reserve, gout, vals_words, vals_scales, size, qs, qrows, old, fade, offs, offs4):
    idx = unstriped(offs)
    idx4 = unstriped(offs4)
    keysu = unpack_weight(keys_words, keys_scales, "e2m1")
    valsu = unpack_weight(vals_words, vals_scales, "e2m1")
    queryq = mxq(f64(query), 0, "e4m3")
    keysidxg = keysu[:, idx]
    a = queryq.T @ keysidxg
    p = np.exp(a - f64(age)[:1][:, idx] * f64(rate))
    z = np.sum(p, axis=1, keepdims=True) + f64(reserve)
    goutq = mxq(f64(gout), 0, "e4m3")
    valsidxg = valsu[:, idx]
    c0 = goutq.T @ valsidxg
    dz = np.sum(c0 * p * f64(size) / np.square(z) * (-1.0), axis=1, keepdims=True)
    dp = c0 / z * f64(size) + dz
    da = dp * p
    gs = da * f64(qs)
    qrowsq = mxq(f64(qrows), 0, "e4m3")
    gsq = mxq(gs, 0, "e4m3")
    gk = qrowsq.T @ gsq
    gf = np.zeros((D, U))
    gf[:, idx4] = gk
    y = f64(old) * f64(fade) + gf
    return y

@@ -1,0 +1,258 @@
+from contextlib import ExitStack
+
+import concourse.mybir as mybir
+from concourse.masks import make_identity
+
+D, E, T, I, Q, U = 512, 512, 1024, 256, 512, 1024
+FLOPS = 3 * 2 * 512 * 512 * 256
+
+F32 = mybir.dt.float32
+BF16 = mybir.dt.bfloat16
+I32 = mybir.dt.int32
+U32 = mybir.dt.uint32
+U16 = mybir.dt.uint16
+U8 = mybir.dt.uint8
+FP8X4 = mybir.dt.float8_e4m3fn_x4
+FP4X4 = mybir.dt.float4_e2m1fn_x4
+ALU = mybir.AluOpType
+ACT = mybir.ActivationFunctionType
+
+P = 128
+PACK = 4
+
+
+def tile_attend_bfadereserve_k_kernel(
+    tc, query, keys_words, keys_scales, age, rate, reserve, gout, vals_words, vals_scales,
+    size, qs, qrows, old, fade, offs, offs4, out,
+):
+    nc = tc.nc
+    with ExitStack() as ctx:
+        lists = ctx.enter_context(tc.tile_pool(name="lists", bufs=1))
+        sb = ctx.enter_context(tc.tile_pool(name="sb", bufs=1))
+        ps = ctx.enter_context(tc.psum_pool(name="ps", bufs=1))
+
+        def tile(name, shape, dtype, tag=None):
+            return sb.tile(shape, dtype, name=name, tag=tag or name, align_bytes=64)
+
+        def bank(name, tag, shape):
+            return ps.tile(shape, F32, name=name, tag=tag)
+
+        offs_t = lists.tile([P, I // 16], U16, name="offs_t")
+        offs4_t = lists.tile([P, I // 16], U16, name="offs4_t")
+
+        key_bytes = tile("key_bytes", [P, T], U8)
+        val_bytes = tile("val_bytes", [P, T], U8)
+        nc.gpsimd.memset(key_bytes[:].bitcast(I32), 0)
+        nc.gpsimd.memset(val_bytes[:].bitcast(I32), 0)
+        rows = tile("rows", [P, P], F32)
+        nc.gpsimd.memset(rows[:], 0.0)
+        ident = tile("ident", [P, P], F32)
+        make_identity(nc, ident[:])
+
+        def load_words(name, words):
+            t = tile(name, [P, T], U16)
+            nc.sync.dma_start(out=t[:].bitcast(I32), in_=words[0].bitcast(I32))
+            return t
+
+        def load_scale_rows(plane, scales):
+            for g in range(4):
+                nc.sync.dma_start(
+                    out=plane[32 * g : 32 * g + 4, :].bitcast(I32),
+                    in_=scales[0, 4 * g : 4 * g + 4, :].bitcast(I32),
+                )
+
+        def load_k_first(name, src):
+            t = tile(name, [P, PACK, src.shape[1]], F32)
+            nc.sync.dma_start(out=t[:], in_=src.rearrange("(p j) w -> p j w", j=PACK))
+            return t
+
+        def load_row_vector(name, src):
+            t = tile(name, [P, PACK], F32)
+            nc.sync.dma_start(out=t[:], in_=src.rearrange("(p r) o -> p (r o)", r=PACK))
+            return t
+
+        nc.sync.dma_start(offs_t[:], offs)
+        key_words = load_words("key_words", keys_words)
+        load_scale_rows(key_bytes, keys_scales)
+        val_words = load_words("val_words", vals_words)
+        query_raw = load_k_first("query_raw", query)
+        load_scale_rows(val_bytes, vals_scales)
+        age_t = tile("age_t", [P, T], F32)
+        nc.sync.dma_start(out=age_t[:], in_=age)
+        rate_t = load_row_vector("rate_t", rate)
+        gout_raw = load_k_first("gout_raw", gout)
+        size_t = tile("size_t", [P, 2], F32)
+        nc.sync.dma_start(out=size_t[:], in_=size.rearrange("o (n c) -> (o n) c", c=2))
+        reserve_t = load_row_vector("reserve_t", reserve)
+        qs_t = load_row_vector("qs_t", qs)
+        qrows_raw = load_k_first("qrows_raw", qrows)
+        nc.sync.dma_start(out=rows[0:8, :], in_=fade.rearrange("o (c n) -> (o c) n", n=P))
+        nc.sync.dma_start(offs4_t[:], offs4)
+        old_half = []
+        for h in range(2):
+            t = tile("old_half%d" % h, [P, 4, 512], F32)
+            nc.sync.dma_start(out=t[:], in_=old[:, 512 * h : 512 * (h + 1)].rearrange("(k m) u -> m k u", m=P))
+            old_half.append(t)
+
+        placed = []
+        for k in range(4):
+            t = tile("placed%d" % k, [P, U], F32)
+            (nc.vector if k < 2 else nc.gpsimd).memset(t[:], 0.0)
+            placed.append(t)
+
+        def gather(name, window, dtype):
+            t = tile(name, [P, I], dtype)
+            nc.vector.tensor_copy(t[:], window[:].indirect(offs_t[:]))
+            return t
+
+        def quantise(name, grouped, width):
+            codes = tile(name + "_codes", [P, width], U32)
+            scales = tile(name + "_scales", [P, width], U8)
+            nc.vector.quantize_mx(out=codes[:].bitcast(FP8X4), scales=scales[:], in_=grouped[:])
+            return codes, scales
+
+        def deal(name, raw, h, on_vector):
+            grouped = tile("%s_bf%d" % (name, h), [P, 2 * P * PACK], BF16)
+            dst = grouped[:].rearrange("p (r s j) -> p s j r", r=2, j=PACK)
+            src = raw[:].rearrange("p j (s r) -> p s j r", r=PACK)[:, :, :, 2 * h : 2 * h + 2]
+            if h in on_vector:
+                nc.vector.tensor_copy(out=dst, in_=src)
+            else:
+                nc.scalar.activation(dst, src, ACT.Copy)
+            return grouped
+
+        def listed_product(name, raw, words, scale_bytes, tags, on_vector):
+            grouped = [deal(name, raw, h, on_vector) for h in range(2)]
+            banks = []
+            for h in range(2):
+                codes, scales = quantise("%s%d" % (name, h), grouped[h], 2 * P)
+                acc = bank("%s_acc%d" % (name, h), tags[h], [P, 2, I])
+                for rr in range(2):
+                    nc.tensor.matmul_mx(
+                        out=acc[:, rr, :],
+                        lhsT=codes[:, P * rr : P * (rr + 1)].bitcast(FP8X4),
+                        lhsT_scale=scales[:, P * rr : P * (rr + 1)],
+                        rhs=words[:].bitcast(FP4X4),
+                        rhs_scale=scale_bytes[:],
+                        start=True,
+                        stop=True,
+                    )
+                banks.append(acc)
+            return banks
+
+        key_g = gather("key_g", key_words, U16)
+        key_sg = gather("key_sg", key_bytes, U8)
+        val_g = gather("val_g", val_words, U16)
+        val_sg = gather("val_sg", val_bytes, U8)
+        score = listed_product("query", query_raw, key_g, key_sg, ["a0", "a1"], [0])
+        age_g = gather("age_g", age_t, F32)
+
+        neg_t = tile("neg_t", [P, PACK, I], F32)
+        p_t = tile("p_t", [P, PACK, I], F32)
+        row_sum = tile("row_sum", [P, PACK], F32)
+        for r in range(PACK):
+            nc.vector.scalar_tensor_tensor(
+                out=neg_t[:, r, :], in0=age_g[:], scalar=rate_t[:, r : r + 1], in1=score[r // 2][:, r % 2, :],
+                op0=ALU.mult, op1=ALU.subtract,
+            )
+            nc.scalar.activation(p_t[:, r, :], neg_t[:, r, :], ACT.Exp, scale=-1.0, accum_out=row_sum[:, r : r + 1])
+
+
+        size_all = bank("size_all", "sz", [P, 2, P])
+        for c in range(2):
+            nc.tensor.transpose(size_all[:, c, :], size_t[:, c : c + 1].to_broadcast([P, P]), ident[:])
+
+        c0 = listed_product("gout", gout_raw, val_g, val_sg, ["c0", "c1"], [0])
+
+        p_size = tile("p_size", [P, PACK, I], F32)
+        for h in range(2):
+            nc.vector.tensor_tensor(
+                p_size[:, 2 * h : 2 * h + 2, :].rearrange("p r (n c) -> p r n c", c=2),
+                p_t[:, 2 * h : 2 * h + 2, :].rearrange("p r (n c) -> p r n c", c=2),
+                size_all[:].rearrange("p c n -> p n c").unsqueeze(1).to_broadcast([P, 2, P, 2]), ALU.mult,
+            )
+        neg_z = tile("neg_z", [P, PACK], F32)
+        neg_zinv = tile("neg_zinv", [P, PACK], F32)
+        qs_z = tile("qs_z", [P, PACK], F32)
+        nc.vector.scalar_tensor_tensor(
+            out=neg_z[:], in0=row_sum[:], scalar=-1.0, in1=reserve_t[:], op0=ALU.mult, op1=ALU.subtract
+        )
+        nc.vector.reciprocal(neg_zinv[:], neg_z[:])
+        nc.vector.scalar_tensor_tensor(
+            out=qs_z[:], in0=qs_t[:], scalar=-1.0, in1=neg_zinv[:], op0=ALU.mult, op1=ALU.mult
+        )
+
+        direct = tile("direct", [P, PACK, I], F32)
+        direct_sum = tile("direct_sum", [P, PACK], F32)
+        back = tile("back", [P, PACK], F32)
+        through_z = tile("through_z", [P, PACK, I], F32)
+        for r in range(PACK):
+            nc.vector.scalar_tensor_tensor(
+                out=direct[:, r, :], in0=c0[r // 2][:, r % 2, :], scalar=qs_z[:, r : r + 1], in1=p_size[:, r, :],
+                op0=ALU.mult, op1=ALU.mult, accum_out=direct_sum[:, r : r + 1],
+            )
+            nc.scalar.activation(back[:, r : r + 1], direct_sum[:, r : r + 1], ACT.Copy, scale=neg_zinv[:, r : r + 1])
+            nc.scalar.activation(through_z[:, r, :], p_t[:, r, :], ACT.Copy, scale=back[:, r : r + 1])
+
+        qrows_q = []
+        for h in range(2):
+            grouped = tile("qrows_bf%d" % h, [P, 2 * P * PACK], BF16, tag=[None, "p_t"][h])
+            nc.scalar.copy(
+                grouped[:].rearrange("p (c i j) -> p c j i", i=4, j=PACK),
+                qrows_raw[:, :, 2 * P * h : 2 * P * (h + 1)].rearrange("p j (c i) -> p c j i", i=4),
+            )
+            qrows_q.append(quantise("qrows%d" % h, grouped, 2 * P))
+
+        gs_bf = tile("gs_bf", [P, I * PACK], BF16)
+        nc.vector.tensor_tensor(
+            gs_bf[:].rearrange("p (c i r) -> p c r i", i=4, r=PACK),
+            direct[:].rearrange("p r (c i) -> p c r i", i=4),
+            through_z[:].rearrange("p r (c i) -> p c r i", i=4),
+            ALU.add,
+        )
+        gs_codes, gs_scales = quantise("gs", gs_bf, I)
+
+        gk = []
+        for h in range(2):
+            codes, scales = qrows_q[h]
+            acc = bank("gk_acc%d" % h, ["a0", "a1"][h], [P, 2, I])
+            for kk in range(2):
+                nc.tensor.matmul_mx(
+                    out=acc[:, kk, :],
+                    lhsT=codes[:, P * kk : P * (kk + 1)].bitcast(FP8X4),
+                    lhsT_scale=scales[:, P * kk : P * (kk + 1)],
+                    rhs=gs_codes[:].bitcast(FP8X4),
+                    rhs_scale=gs_scales[:],
+                    start=True,
+                    stop=True,
+                )
+            for kk in range(2):
+                t = tile("gk%d" % (2 * h + kk), [P, I], F32)
+                nc.scalar.copy(t[:], acc[:, kk, :])
+                gk.append(t)
+
+        turned = bank("turned", "x1", [P, P])
+        nc.tensor.transpose(turned[:], rows[:], ident[:])
+        cols = tile("cols", [P, 8], F32)
+        nc.scalar.copy(cols[:], turned[:, 0:8])
+        faded_t = []
+        for c in range(8):
+            stage = bank("stage%d" % c, "x%d" % (c % 2), [P, 4, P])
+            for k in range(4):
+                nc.tensor.transpose(stage[:, k, :], old_half[c // 4][:, k, P * (c % 4) : P * (c % 4 + 1)], ident[:])
+            t = tile("faded_t%d" % c, [P, D], F32, tag={0: "direct", 1: "through_z"}.get(c))
+            nc.scalar.activation(t[:], stage[:].rearrange("p k m -> p (k m)"), ACT.Copy, scale=cols[:, c : c + 1])
+            faded_t.append(t)
+
+        ring = ["y0", "c0", "c1", "sz", "a0", "a1"]
+        for k in range(4):
+            nc.vector.tensor_copy(placed[k][:].indirect(offs4_t[:]), gk[k][:])
+            for h in range(2):
+                faded = bank("faded%d_%d" % (k, h), ring[(2 * k + h) % len(ring)], [P, 4, P])
+                for cc in range(4):
+                    nc.tensor.transpose(faded[:, cc, :], faded_t[4 * h + cc][:, P * k : P * (k + 1)], ident[:])
+                res = tile("res%d_%d" % (k, h), [P, 512], F32)
+                nc.vector.tensor_tensor(
+                    res[:], faded[:].rearrange("p c n -> p (c n)"), placed[k][:, 512 * h : 512 * (h + 1)], ALU.add
+                )
+                nc.sync.dma_start(out=out[P * k : P * (k + 1), 512 * h : 512 * (h + 1)], in_=res[:])

@@ -19,6 +19,7 @@ ACT = mybir.ActivationFunctionType
 
 P = 128
 PACK = 4
+NG = 2
 
 
 def tile_attend_bfadereserve_k_kernel(
@@ -42,12 +43,12 @@ def tile_attend_bfadereserve_k_kernel(
 
         key_bytes = tile("key_bytes", [P, T], U8)
         val_bytes = tile("val_bytes", [P, T], U8)
-        nc.gpsimd.memset(key_bytes[:].bitcast(I32), 0)
-        nc.gpsimd.memset(val_bytes[:].bitcast(I32), 0)
         rows = tile("rows", [P, P], F32)
-        nc.gpsimd.memset(rows[:], 0.0)
         ident = tile("ident", [P, P], F32)
+        nc.gpsimd.memset(rows[:], 0.0)
+        nc.gpsimd.memset(key_bytes[:].bitcast(I32), 0)
         make_identity(nc, ident[:])
+        nc.gpsimd.memset(val_bytes[:].bitcast(I32), 0)
 
         def load_words(name, words):
             t = tile(name, [P, T], U16)
@@ -72,30 +73,35 @@ def tile_attend_bfadereserve_k_kernel(
             return t
 
         nc.sync.dma_start(offs_t[:], offs)
+        nc.sync.dma_start(out=rows[0:8, :], in_=fade.rearrange("o (c n) -> (o c) n", n=P))
         key_words = load_words("key_words", keys_words)
         load_scale_rows(key_bytes, keys_scales)
-        val_words = load_words("val_words", vals_words)
         query_raw = load_k_first("query_raw", query)
-        load_scale_rows(val_bytes, vals_scales)
         age_t = tile("age_t", [P, T], F32)
         nc.sync.dma_start(out=age_t[:], in_=age)
+        val_words = load_words("val_words", vals_words)
         rate_t = load_row_vector("rate_t", rate)
-        gout_raw = load_k_first("gout_raw", gout)
         size_t = tile("size_t", [P, 2], F32)
         nc.sync.dma_start(out=size_t[:], in_=size.rearrange("o (n c) -> (o n) c", c=2))
-        reserve_t = load_row_vector("reserve_t", reserve)
         qs_t = load_row_vector("qs_t", qs)
+        gout_raw = load_k_first("gout_raw", gout)
+        reserve_t = load_row_vector("reserve_t", reserve)
+        load_scale_rows(val_bytes, vals_scales)
         qrows_raw = load_k_first("qrows_raw", qrows)
-        nc.sync.dma_start(out=rows[0:8, :], in_=fade.rearrange("o (c n) -> (o c) n", n=P))
-        nc.sync.dma_start(offs4_t[:], offs4)
         old_half = []
         for h in range(2):
-            t = tile("old_half%d" % h, [P, 4, 512], F32)
-            nc.sync.dma_start(out=t[:], in_=old[:, 512 * h : 512 * (h + 1)].rearrange("(k m) u -> m k u", m=P))
+            t = tile("old_half%d" % h, [P, 4 - NG, 512], F32)
+            nc.sync.dma_start(out=t[:], in_=old[P * NG :, 512 * h : 512 * (h + 1)].rearrange("(k m) u -> m k u", m=P))
             old_half.append(t)
+        nc.sync.dma_start(offs4_t[:], offs4)
+        old_rows = []
+        for k in range(NG):
+            t = tile("old_rows%d" % k, [P, U], F32)
+            nc.sync.dma_start(out=t[:], in_=old[P * k : P * (k + 1), :])
+            old_rows.append(t)
 
         placed = []
-        for k in range(4):
+        for k in range(3):
             t = tile("placed%d" % k, [P, U], F32)
             (nc.vector if k < 2 else nc.gpsimd).memset(t[:], 0.0)
             placed.append(t)
@@ -105,11 +111,23 @@ def tile_attend_bfadereserve_k_kernel(
             nc.vector.tensor_copy(t[:], window[:].indirect(offs_t[:]))
             return t
 
-        def quantise(name, grouped, width):
-            codes = tile(name + "_codes", [P, width], U32)
-            scales = tile(name + "_scales", [P, width], U8)
-            nc.vector.quantize_mx(out=codes[:].bitcast(FP8X4), scales=scales[:], in_=grouped[:])
-            return codes, scales
+        def planes(name, width, tag=None):
+            return tile(name + "_codes", [P, width], U32, tag=tag), tile(name + "_scales", [P, width], U8)
+
+        def quantise(operand, cols, grouped):
+            codes, scales = operand
+            nc.vector.quantize_mx(out=codes[:, cols].bitcast(FP8X4), scales=scales[:, cols], in_=grouped[:])
+
+        def product(acc, stationary, s_cols, moving, m_cols, moving_dtype):
+            nc.tensor.matmul_mx(
+                out=acc,
+                lhsT=stationary[0][:, s_cols].bitcast(FP8X4),
+                lhsT_scale=stationary[1][:, s_cols],
+                rhs=moving[0][:, m_cols].bitcast(moving_dtype),
+                rhs_scale=moving[1][:, m_cols],
+                start=True,
+                stop=True,
+            )
 
         def deal(name, raw, h, on_vector):
             grouped = tile("%s_bf%d" % (name, h), [P, 2 * P * PACK], BF16)
@@ -121,30 +139,36 @@ def tile_attend_bfadereserve_k_kernel(
                 nc.scalar.activation(dst, src, ACT.Copy)
             return grouped
 
-        def listed_product(name, raw, words, scale_bytes, tags, on_vector):
-            grouped = [deal(name, raw, h, on_vector) for h in range(2)]
+        def listed_product(name, grouped, words, scale_bytes, tags, codes_tag=None):
+            operand = planes(name, Q, codes_tag)
             banks = []
             for h in range(2):
-                codes, scales = quantise("%s%d" % (name, h), grouped[h], 2 * P)
+                quantise(operand, slice(2 * P * h, 2 * P * (h + 1)), grouped[h])
                 acc = bank("%s_acc%d" % (name, h), tags[h], [P, 2, I])
                 for rr in range(2):
-                    nc.tensor.matmul_mx(
-                        out=acc[:, rr, :],
-                        lhsT=codes[:, P * rr : P * (rr + 1)].bitcast(FP8X4),
-                        lhsT_scale=scales[:, P * rr : P * (rr + 1)],
-                        rhs=words[:].bitcast(FP4X4),
-                        rhs_scale=scale_bytes[:],
-                        start=True,
-                        stop=True,
-                    )
+                    r = 2 * h + rr
+                    product(acc[:, rr, :], operand, slice(P * r, P * (r + 1)), (words, scale_bytes), slice(0, I), FP4X4)
                 banks.append(acc)
             return banks
 
         key_g = gather("key_g", key_words, U16)
         key_sg = gather("key_sg", key_bytes, U8)
+        turned = bank("turned", "x1", [P, P])
+        nc.tensor.transpose(turned[:], rows[:], ident[:])
+        cols = tile("cols", [P, 8], F32)
+        nc.scalar.copy(cols[:], turned[:, 0:8])
+
+        fade_all = tile("fade_all", [P, U], F32)
+        for h in range(2):
+            spread = bank("spread%d" % h, "x%d" % h, [P, 4, P])
+            for cc in range(4):
+                c = 4 * h + cc
+                nc.tensor.transpose(spread[:, cc, :], cols[:, c : c + 1].to_broadcast([P, P]), ident[:])
+            nc.scalar.copy(fade_all[:, 512 * h : 512 * (h + 1)], spread[:].rearrange("p c n -> p (c n)"))
+
         val_g = gather("val_g", val_words, U16)
-        val_sg = gather("val_sg", val_bytes, U8)
-        score = listed_product("query", query_raw, key_g, key_sg, ["a0", "a1"], [0])
+        query_bf = [deal("query", query_raw, h, [0]) for h in range(2)]
+        score = listed_product("query", query_bf, key_g, key_sg, ["a0", "a1"])
         age_g = gather("age_g", age_t, F32)
 
         neg_t = tile("neg_t", [P, PACK, I], F32)
@@ -162,97 +186,109 @@ def tile_attend_bfadereserve_k_kernel(
         for c in range(2):
             nc.tensor.transpose(size_all[:, c, :], size_t[:, c : c + 1].to_broadcast([P, P]), ident[:])
 
-        c0 = listed_product("gout", gout_raw, val_g, val_sg, ["c0", "c1"], [0])
+        z = tile("z", [P, PACK], F32)
+        z_inv = tile("z_inv", [P, PACK], F32)
+        nc.vector.tensor_tensor(z[:], row_sum[:], reserve_t[:], ALU.add)
+        nc.vector.reciprocal(z_inv[:], z[:])
+
+        gout_bf = [deal("gout", gout_raw, h, []) for h in range(2)]
+        val_sg = gather("val_sg", val_bytes, U8)
+        c0 = listed_product("gout", gout_bf, val_g, val_sg, ["c0", "c1"], codes_tag="val_bytes")
 
         p_size = tile("p_size", [P, PACK, I], F32)
-        for h in range(2):
-            nc.vector.tensor_tensor(
-                p_size[:, 2 * h : 2 * h + 2, :].rearrange("p r (n c) -> p r n c", c=2),
-                p_t[:, 2 * h : 2 * h + 2, :].rearrange("p r (n c) -> p r n c", c=2),
-                size_all[:].rearrange("p c n -> p n c").unsqueeze(1).to_broadcast([P, 2, P, 2]), ALU.mult,
+        for r in range(PACK):
+            nc.vector.scalar_tensor_tensor(
+                out=p_size[:, r, :].rearrange("p (n c) -> p n c", c=2),
+                in0=p_t[:, r, :].rearrange("p (n c) -> p n c", c=2),
+                scalar=qs_t[:, r : r + 1],
+                in1=size_all[:].rearrange("p c n -> p n c"),
+                op0=ALU.mult, op1=ALU.mult,
             )
-        neg_z = tile("neg_z", [P, PACK], F32)
-        neg_zinv = tile("neg_zinv", [P, PACK], F32)
-        qs_z = tile("qs_z", [P, PACK], F32)
-        nc.vector.scalar_tensor_tensor(
-            out=neg_z[:], in0=row_sum[:], scalar=-1.0, in1=reserve_t[:], op0=ALU.mult, op1=ALU.subtract
-        )
-        nc.vector.reciprocal(neg_zinv[:], neg_z[:])
-        nc.vector.scalar_tensor_tensor(
-            out=qs_z[:], in0=qs_t[:], scalar=-1.0, in1=neg_zinv[:], op0=ALU.mult, op1=ALU.mult
-        )
 
         direct = tile("direct", [P, PACK, I], F32)
         direct_sum = tile("direct_sum", [P, PACK], F32)
-        back = tile("back", [P, PACK], F32)
         through_z = tile("through_z", [P, PACK, I], F32)
         for r in range(PACK):
             nc.vector.scalar_tensor_tensor(
-                out=direct[:, r, :], in0=c0[r // 2][:, r % 2, :], scalar=qs_z[:, r : r + 1], in1=p_size[:, r, :],
+                out=direct[:, r, :], in0=c0[r // 2][:, r % 2, :], scalar=z_inv[:, r : r + 1], in1=p_size[:, r, :],
                 op0=ALU.mult, op1=ALU.mult, accum_out=direct_sum[:, r : r + 1],
             )
-            nc.scalar.activation(back[:, r : r + 1], direct_sum[:, r : r + 1], ACT.Copy, scale=neg_zinv[:, r : r + 1])
-            nc.scalar.activation(through_z[:, r, :], p_t[:, r, :], ACT.Copy, scale=back[:, r : r + 1])
+        for r in range(PACK):
+            nc.vector.tensor_scalar(
+                through_z[:, r, :], p_t[:, r, :], direct_sum[:, r : r + 1], z_inv[:, r : r + 1], ALU.mult, ALU.mult
+            )
 
-        qrows_q = []
+        qrows_q = planes("qrows", D)
         for h in range(2):
-            grouped = tile("qrows_bf%d" % h, [P, 2 * P * PACK], BF16, tag=[None, "p_t"][h])
+            grouped = tile("qrows_bf%d" % h, [P, 2 * P * PACK], BF16)
             nc.scalar.copy(
                 grouped[:].rearrange("p (c i j) -> p c j i", i=4, j=PACK),
                 qrows_raw[:, :, 2 * P * h : 2 * P * (h + 1)].rearrange("p j (c i) -> p c j i", i=4),
             )
-            qrows_q.append(quantise("qrows%d" % h, grouped, 2 * P))
+            quantise(qrows_q, slice(2 * P * h, 2 * P * (h + 1)), grouped)
 
-        gs_bf = tile("gs_bf", [P, I * PACK], BF16)
-        nc.vector.tensor_tensor(
-            gs_bf[:].rearrange("p (c i r) -> p c r i", i=4, r=PACK),
-            direct[:].rearrange("p r (c i) -> p c r i", i=4),
-            through_z[:].rearrange("p r (c i) -> p c r i", i=4),
-            ALU.add,
-        )
-        gs_codes, gs_scales = quantise("gs", gs_bf, I)
+        gs_q = planes("gs", I)
+        for b in range(2):
+            slots = slice(P * b, P * (b + 1))
+            gs_bf = tile("gs_bf%d" % b, [P, P * PACK], BF16, tag="qrows_bf%d" % b)
+            nc.vector.tensor_tensor(
+                gs_bf[:].rearrange("p (c i r) -> p c r i", i=4, r=PACK),
+                direct[:, :, slots].rearrange("p r (c i) -> p c r i", i=4),
+                through_z[:, :, slots].rearrange("p r (c i) -> p c r i", i=4),
+                ALU.subtract,
+            )
+            quantise(gs_q, slots, gs_bf)
 
-        gk = []
-        for h in range(2):
-            codes, scales = qrows_q[h]
-            acc = bank("gk_acc%d" % h, ["a0", "a1"][h], [P, 2, I])
-            for kk in range(2):
-                nc.tensor.matmul_mx(
-                    out=acc[:, kk, :],
-                    lhsT=codes[:, P * kk : P * (kk + 1)].bitcast(FP8X4),
-                    lhsT_scale=scales[:, P * kk : P * (kk + 1)],
-                    rhs=gs_codes[:].bitcast(FP8X4),
-                    rhs_scale=gs_scales[:],
-                    start=True,
-                    stop=True,
-                )
-            for kk in range(2):
-                t = tile("gk%d" % (2 * h + kk), [P, I], F32)
-                nc.scalar.copy(t[:], acc[:, kk, :])
-                gk.append(t)
+        gk = [tile("gk%d" % k, [P, I], F32) for k in range(4)]
+        pieces = [(0, 0, P), (1, 0, P), (0, P, I), (1, P, I), (2, 0, I), (3, 0, I)]
+        for (k, lo, hi), tag in zip(pieces, ["a0", "a1", "c0", "c1", "sz", "y0"]):
+            acc = bank("gk_acc%d_%d" % (k, lo), tag, [P, hi - lo])
+            product(acc[:], qrows_q, slice(P * k, P * (k + 1)), gs_q, slice(lo, hi), FP8X4)
+            nc.scalar.copy(gk[k][:, lo:hi], acc[:])
 
-        turned = bank("turned", "x1", [P, P])
-        nc.tensor.transpose(turned[:], rows[:], ident[:])
-        cols = tile("cols", [P, 8], F32)
-        nc.scalar.copy(cols[:], turned[:, 0:8])
+        def scatter(k, lo, hi):
+            window = placed[min(k, 2)]
+            nc.vector.tensor_copy(window[:].indirect(offs4_t[:, lo // 16 : hi // 16]), gk[k][:, lo:hi])
+
+        for k, lo, hi in pieces[:4]:
+            scatter(k, lo, hi)
+
+        faded_g = tile("faded_g", [P, NG, U], F32, tag="qrows_bf1")
+
+        def fade_rows(k, lo, hi):
+            nc.gpsimd.tensor_tensor(faded_g[:, k, lo:hi], old_rows[k][:, lo:hi], fade_all[:, lo:hi], ALU.mult)
+
+        def finish_rows(k, lo, hi):
+            res = tile("res%d_%d" % (k, lo), [P, hi - lo], F32)
+            nc.gpsimd.tensor_tensor(res[:], faded_g[:, k, lo:hi], placed[k][:, lo:hi], ALU.add)
+            nc.scalar.dma_start(out=out[P * k : P * (k + 1), lo:hi], in_=res[:])
+
+        fade_rows(0, 0, U)
+        fade_rows(1, 0, 512)
+        finish_rows(0, 0, 512)
+        fade_rows(1, 512, U)
+        finish_rows(0, 512, U)
+        finish_rows(1, 0, 512)
+        finish_rows(1, 512, U)
+
         faded_t = []
         for c in range(8):
-            stage = bank("stage%d" % c, "x%d" % (c % 2), [P, 4, P])
-            for k in range(4):
+            stage = bank("stage%d" % c, "x%d" % (c % 2), [P, 4 - NG, P])
+            for k in range(4 - NG):
                 nc.tensor.transpose(stage[:, k, :], old_half[c // 4][:, k, P * (c % 4) : P * (c % 4 + 1)], ident[:])
-            t = tile("faded_t%d" % c, [P, D], F32, tag={0: "direct", 1: "through_z"}.get(c))
+            t = tile("faded_t%d" % c, [P, (4 - NG) * P], F32)
             nc.scalar.activation(t[:], stage[:].rearrange("p k m -> p (k m)"), ACT.Copy, scale=cols[:, c : c + 1])
             faded_t.append(t)
 
-        ring = ["y0", "c0", "c1", "sz", "a0", "a1"]
-        for k in range(4):
-            nc.vector.tensor_copy(placed[k][:].indirect(offs4_t[:]), gk[k][:])
+        ring = ["a0", "a1", "c0", "c1"]
+        for k in range(4 - NG):
+            scatter(NG + k, 0, I)
             for h in range(2):
-                faded = bank("faded%d_%d" % (k, h), ring[(2 * k + h) % len(ring)], [P, 4, P])
+                faded = bank("faded%d_%d" % (k, h), ring[2 * k + h], [P, 4, P])
                 for cc in range(4):
                     nc.tensor.transpose(faded[:, cc, :], faded_t[4 * h + cc][:, P * k : P * (k + 1)], ident[:])
-                res = tile("res%d_%d" % (k, h), [P, 512], F32)
+                res = tile("res%d_%d" % (NG + k, h), [P, 512], F32)
                 nc.vector.tensor_tensor(
-                    res[:], faded[:].rearrange("p c n -> p (c n)"), placed[k][:, 512 * h : 512 * (h + 1)], ALU.add
+                    res[:], faded[:].rearrange("p c n -> p (c n)"), placed[2][:, 512 * h : 512 * (h + 1)], ALU.add
                 )
-                nc.sync.dma_start(out=out[P * k : P * (k + 1), 512 * h : 512 * (h + 1)], in_=res[:])
+                nc.sync.dma_start(out=out[P * (NG + k) : P * (NG + k + 1), 512 * h : 512 * (h + 1)], in_=res[:])

@@ -19,7 +19,7 @@ ACT = mybir.ActivationFunctionType
 
 P = 128
 PACK = 4
-NG = 2
+NG = 1
 
 
 def tile_attend_bfadereserve_k_kernel(
@@ -84,24 +84,20 @@ def tile_attend_bfadereserve_k_kernel(
         size_t = tile("size_t", [P, 2], F32)
         nc.sync.dma_start(out=size_t[:], in_=size.rearrange("o (n c) -> (o n) c", c=2))
         qs_t = load_row_vector("qs_t", qs)
-        gout_raw = load_k_first("gout_raw", gout)
         reserve_t = load_row_vector("reserve_t", reserve)
+        gout_raw = load_k_first("gout_raw", gout)
         load_scale_rows(val_bytes, vals_scales)
         qrows_raw = load_k_first("qrows_raw", qrows)
+        old_first = tile("old_first", [P, U], F32)
+        nc.sync.dma_start(out=old_first[:], in_=old[0:P, :])
         old_half = []
         for h in range(2):
             t = tile("old_half%d" % h, [P, 4 - NG, 512], F32)
             nc.sync.dma_start(out=t[:], in_=old[P * NG :, 512 * h : 512 * (h + 1)].rearrange("(k m) u -> m k u", m=P))
             old_half.append(t)
         nc.sync.dma_start(offs4_t[:], offs4)
-        old_rows = []
-        for k in range(NG):
-            t = tile("old_rows%d" % k, [P, U], F32)
-            nc.sync.dma_start(out=t[:], in_=old[P * k : P * (k + 1), :])
-            old_rows.append(t)
-
         placed = []
-        for k in range(3):
+        for k in range(4):
             t = tile("placed%d" % k, [P, U], F32)
             (nc.vector if k < 2 else nc.gpsimd).memset(t[:], 0.0)
             placed.append(t)
@@ -230,7 +226,7 @@ def tile_attend_bfadereserve_k_kernel(
         gs_q = planes("gs", I)
         for b in range(2):
             slots = slice(P * b, P * (b + 1))
-            gs_bf = tile("gs_bf%d" % b, [P, P * PACK], BF16, tag="qrows_bf%d" % b)
+            gs_bf = tile("gs_bf%d" % b, [P, P * PACK], BF16, tag="qrows_bf0")
             nc.vector.tensor_tensor(
                 gs_bf[:].rearrange("p (c i r) -> p c r i", i=4, r=PACK),
                 direct[:, :, slots].rearrange("p r (c i) -> p c r i", i=4),
@@ -239,56 +235,64 @@ def tile_attend_bfadereserve_k_kernel(
             )
             quantise(gs_q, slots, gs_bf)
 
-        gk = [tile("gk%d" % k, [P, I], F32) for k in range(4)]
-        pieces = [(0, 0, P), (1, 0, P), (0, P, I), (1, P, I), (2, 0, I), (3, 0, I)]
-        for (k, lo, hi), tag in zip(pieces, ["a0", "a1", "c0", "c1", "sz", "y0"]):
-            acc = bank("gk_acc%d_%d" % (k, lo), tag, [P, hi - lo])
-            product(acc[:], qrows_q, slice(P * k, P * (k + 1)), gs_q, slice(lo, hi), FP8X4)
-            nc.scalar.copy(gk[k][:, lo:hi], acc[:])
-
-        def scatter(k, lo, hi):
-            window = placed[min(k, 2)]
-            nc.vector.tensor_copy(window[:].indirect(offs4_t[:, lo // 16 : hi // 16]), gk[k][:, lo:hi])
-
-        for k, lo, hi in pieces[:4]:
-            scatter(k, lo, hi)
-
-        faded_g = tile("faded_g", [P, NG, U], F32, tag="qrows_bf1")
-
-        def fade_rows(k, lo, hi):
-            nc.gpsimd.tensor_tensor(faded_g[:, k, lo:hi], old_rows[k][:, lo:hi], fade_all[:, lo:hi], ALU.mult)
-
-        def finish_rows(k, lo, hi):
-            res = tile("res%d_%d" % (k, lo), [P, hi - lo], F32)
-            nc.gpsimd.tensor_tensor(res[:], faded_g[:, k, lo:hi], placed[k][:, lo:hi], ALU.add)
-            nc.scalar.dma_start(out=out[P * k : P * (k + 1), lo:hi], in_=res[:])
-
-        fade_rows(0, 0, U)
-        fade_rows(1, 0, 512)
-        finish_rows(0, 0, 512)
-        fade_rows(1, 512, U)
-        finish_rows(0, 512, U)
-        finish_rows(1, 0, 512)
-        finish_rows(1, 512, U)
-
         faded_t = []
-        for c in range(8):
-            stage = bank("stage%d" % c, "x%d" % (c % 2), [P, 4 - NG, P])
+
+        def fade_turned(c):
+            stage = bank("stage%d" % c, ["x0", "x1", "y0", "sz", "x0", "x1", "x0", "x1"][c], [P, 4 - NG, P])
             for k in range(4 - NG):
                 nc.tensor.transpose(stage[:, k, :], old_half[c // 4][:, k, P * (c % 4) : P * (c % 4 + 1)], ident[:])
             t = tile("faded_t%d" % c, [P, (4 - NG) * P], F32)
             nc.scalar.activation(t[:], stage[:].rearrange("p k m -> p (k m)"), ACT.Copy, scale=cols[:, c : c + 1])
             faded_t.append(t)
 
-        ring = ["a0", "a1", "c0", "c1"]
-        for k in range(4 - NG):
-            scatter(NG + k, 0, I)
-            for h in range(2):
-                faded = bank("faded%d_%d" % (k, h), ring[2 * k + h], [P, 4, P])
-                for cc in range(4):
-                    nc.tensor.transpose(faded[:, cc, :], faded_t[4 * h + cc][:, P * k : P * (k + 1)], ident[:])
-                res = tile("res%d_%d" % (NG + k, h), [P, 512], F32)
-                nc.vector.tensor_tensor(
-                    res[:], faded[:].rearrange("p c n -> p (c n)"), placed[2][:, 512 * h : 512 * (h + 1)], ALU.add
-                )
-                nc.sync.dma_start(out=out[P * (NG + k) : P * (NG + k + 1), 512 * h : 512 * (h + 1)], in_=res[:])
+        gk = {}
+
+        def key_gradient(tag, pieces):
+            acc = bank("gk_acc%d_%d" % pieces[0][:2], tag, [P, 512])
+            places = []
+            for k, lo, hi in pieces:
+                start = sum(b - a for a, b in places)
+                places.append((start, start + hi - lo))
+                product(acc[:, start : start + hi - lo], qrows_q, slice(P * k, P * (k + 1)), gs_q, slice(lo, hi), FP8X4)
+            for (k, lo, hi), (a, b) in zip(pieces, places):
+                gk[k, lo] = tile("gk%d_%d" % (k, lo), [P, hi - lo], F32)
+                nc.scalar.copy(gk[k, lo][:], acc[:, a:b])
+
+        for c in range(6):
+            fade_turned(c)
+        key_gradient("x0", [(0, 0, P)])
+        key_gradient("x1", [(0, P, I), (1, 0, I)])
+        fade_turned(6)
+        fade_turned(7)
+        key_gradient("x0", [(2, 0, I), (3, 0, I)])
+
+        for k, lo, hi in [(0, 0, P), (0, P, I), (1, 0, I), (2, 0, I), (3, 0, I)]:
+            nc.vector.tensor_copy(placed[k][:].indirect(offs4_t[:, lo // 16 : hi // 16]), gk[k, lo][:])
+
+        def finish(engine, queue, k, h, faded, tag=None):
+            half = slice(512 * h, 512 * (h + 1))
+            res = tile("res%d_%d" % (k, h), [P, 512], F32, tag=tag)
+            engine.tensor_tensor(res[:], faded, placed[k][:, half], ALU.add)
+            queue.dma_start(out=out[P * k : P * (k + 1), half], in_=res[:])
+
+        faded_first = []
+        for h in range(2):
+            half = slice(512 * h, 512 * (h + 1))
+            t = tile("faded_first%d" % h, [P, 512], F32, tag=["gout_bf1", "qrows_bf0"][h])
+            nc.gpsimd.tensor_tensor(t[:], old_first[:, half], fade_all[:, half], ALU.mult)
+            faded_first.append(t)
+        for h in range(2):
+            finish(nc.gpsimd, nc.sync, 0, h, faded_first[h][:])
+
+        ring = ["a0", "x1", "x0", "a1", "c0", "c1"]
+        for n, (k, h) in enumerate([(1, 0), (1, 1), (2, 0), (2, 1), (3, 0), (3, 1)]):
+            faded = bank("faded%d_%d" % (k, h), ring[n], [P, 4, P])
+            for cc in range(4):
+                nc.tensor.transpose(faded[:, cc, :], faded_t[4 * h + cc][:, P * (k - 1) : P * k], ident[:])
+            flat = faded[:].rearrange("p c n -> p (c n)")
+            if n < 3:
+                moved = tile("moved%d" % n, [P, 512], F32, tag=["gk0_0", None, None][n])
+                nc.scalar.copy(moved[:], flat)
+                finish(nc.gpsimd, nc.sync, k, h, moved[:])
+            else:
+                finish(nc.vector, nc.scalar, k, h, flat, tag={3: "gk3_0"}.get(n))

@@ -238,7 +238,7 @@ def tile_attend_bfadereserve_k_kernel(
         faded_t = []
 
         def fade_turned(c):
-            stage = bank("stage%d" % c, ["x0", "x1", "y0", "sz", "x0", "x1", "x0", "x1"][c], [P, 4 - NG, P])
+            stage = bank("stage%d" % c, ["x0", "x1", "y0", "sz", "x0", "x1", "x1", "x1"][c], [P, 4 - NG, P])
             for k in range(4 - NG):
                 nc.tensor.transpose(stage[:, k, :], old_half[c // 4][:, k, P * (c % 4) : P * (c % 4 + 1)], ident[:])
             t = tile("faded_t%d" % c, [P, (4 - NG) * P], F32)
@@ -260,20 +260,25 @@ def tile_attend_bfadereserve_k_kernel(
 
         for c in range(6):
             fade_turned(c)
-        key_gradient("x0", [(0, 0, P)])
-        key_gradient("x1", [(0, P, I), (1, 0, I)])
+        key_gradient("x0", [(0, 0, P), (1, 0, P)])
+        key_gradient("x1", [(0, P, I), (1, P, I)])
+        key_gradient("x0", [(2, 0, I), (3, 0, I)])
         fade_turned(6)
         fade_turned(7)
-        key_gradient("x0", [(2, 0, I), (3, 0, I)])
 
-        for k, lo, hi in [(0, 0, P), (0, P, I), (1, 0, I), (2, 0, I), (3, 0, I)]:
+        for k, lo, hi in [(0, 0, P), (1, 0, P), (0, P, I), (1, P, I), (2, 0, I), (3, 0, I)]:
             nc.vector.tensor_copy(placed[k][:].indirect(offs4_t[:, lo // 16 : hi // 16]), gk[k, lo][:])
 
-        def finish(engine, queue, k, h, faded, tag=None):
+        def finish(engine, queue, k, h, faded, res):
             half = slice(512 * h, 512 * (h + 1))
-            res = tile("res%d_%d" % (k, h), [P, 512], F32, tag=tag)
-            engine.tensor_tensor(res[:], faded, placed[k][:, half], ALU.add)
-            queue.dma_start(out=out[P * k : P * (k + 1), half], in_=res[:])
+            engine.tensor_tensor(res, faded, placed[k][:, half], ALU.add)
+            queue.dma_start(out=out[P * k : P * (k + 1), half], in_=res)
+
+        def turned_back(k, h, tag):
+            faded = bank("faded%d_%d" % (k, h), tag, [P, 4, P])
+            for cc in range(4):
+                nc.tensor.transpose(faded[:, cc, :], faded_t[4 * h + cc][:, P * (k - 1) : P * k], ident[:])
+            return faded[:].rearrange("p c n -> p (c n)")
 
         faded_first = []
         for h in range(2):
@@ -282,17 +287,16 @@ def tile_attend_bfadereserve_k_kernel(
             nc.gpsimd.tensor_tensor(t[:], old_first[:, half], fade_all[:, half], ALU.mult)
             faded_first.append(t)
         for h in range(2):
-            finish(nc.gpsimd, nc.sync, 0, h, faded_first[h][:])
+            res = tile("res0_%d" % h, [P, 512], F32)
+            finish(nc.gpsimd, nc.sync, 0, h, faded_first[h][:], res[:])
 
-        ring = ["a0", "x1", "x0", "a1", "c0", "c1"]
-        for n, (k, h) in enumerate([(1, 0), (1, 1), (2, 0), (2, 1), (3, 0), (3, 1)]):
-            faded = bank("faded%d_%d" % (k, h), ring[n], [P, 4, P])
-            for cc in range(4):
-                nc.tensor.transpose(faded[:, cc, :], faded_t[4 * h + cc][:, P * (k - 1) : P * k], ident[:])
-            flat = faded[:].rearrange("p c n -> p (c n)")
-            if n < 3:
-                moved = tile("moved%d" % n, [P, 512], F32, tag=["gk0_0", None, None][n])
-                nc.scalar.copy(moved[:], flat)
-                finish(nc.gpsimd, nc.sync, k, h, moved[:])
-            else:
-                finish(nc.vector, nc.scalar, k, h, flat, tag={3: "gk3_0"}.get(n))
+        for h in range(2):
+            moved = tile("moved%d" % h, [P, 512], F32)
+            nc.scalar.copy(moved[:], turned_back(1, h, "x%d" % h))
+            res = tile("res1_%d" % h, [P, 512], F32)
+            finish(nc.gpsimd, [nc.sync, nc.scalar][h], 1, h, moved[:], res[:])
+
+        res_last = tile("res_last", [P, 4, 512], F32, tag="moved0")
+        for n, tag in enumerate(["a0", "a1", "c0", "c1"]):
+            k, h = 2 + n // 2, n % 2
+            finish(nc.vector, nc.sync, k, h, turned_back(k, h, tag), res_last[:, n, :])

from contextlib import ExitStack

import concourse.mybir as mybir
from concourse.masks import make_identity

D, E, T, I, Q, U = 512, 512, 1024, 256, 512, 1024
FLOPS = 3 * 2 * 512 * 512 * 256

F32 = mybir.dt.float32
BF16 = mybir.dt.bfloat16
I32 = mybir.dt.int32
U32 = mybir.dt.uint32
U16 = mybir.dt.uint16
U8 = mybir.dt.uint8
FP8X4 = mybir.dt.float8_e4m3fn_x4
FP4X4 = mybir.dt.float4_e2m1fn_x4
ALU = mybir.AluOpType
ACT = mybir.ActivationFunctionType

P = 128
PACK = 4
NG = 1


def tile_attend_bfadereserve_k_kernel(
    tc, query, keys_words, keys_scales, age, rate, reserve, gout, vals_words, vals_scales,
    size, qs, qrows, old, fade, offs, offs4, out,
):
    nc = tc.nc
    with ExitStack() as ctx:
        lists = ctx.enter_context(tc.tile_pool(name="lists", bufs=1))
        sb = ctx.enter_context(tc.tile_pool(name="sb", bufs=1))
        ps = ctx.enter_context(tc.psum_pool(name="ps", bufs=1))

        def tile(name, shape, dtype, tag=None):
            return sb.tile(shape, dtype, name=name, tag=tag or name, align_bytes=64)

        def bank(name, tag, shape):
            return ps.tile(shape, F32, name=name, tag=tag)

        offs_t = lists.tile([P, I // 16], U16, name="offs_t")
        offs4_t = lists.tile([P, I // 16], U16, name="offs4_t")

        key_bytes = tile("key_bytes", [P, T], U8)
        val_bytes = tile("val_bytes", [P, T], U8)
        rows = tile("rows", [P, P], F32)
        ident = tile("ident", [P, P], F32)
        nc.gpsimd.memset(rows[:], 0.0)
        nc.gpsimd.memset(key_bytes[:].bitcast(I32), 0)
        make_identity(nc, ident[:])
        nc.gpsimd.memset(val_bytes[:].bitcast(I32), 0)

        def load_words(name, words):
            t = tile(name, [P, T], U16)
            nc.sync.dma_start(out=t[:].bitcast(I32), in_=words[0].bitcast(I32))
            return t

        def load_scale_rows(plane, scales):
            for g in range(4):
                nc.sync.dma_start(
                    out=plane[32 * g : 32 * g + 4, :].bitcast(I32),
                    in_=scales[0, 4 * g : 4 * g + 4, :].bitcast(I32),
                )

        def load_k_first(name, src):
            t = tile(name, [P, PACK, src.shape[1]], F32)
            nc.sync.dma_start(out=t[:], in_=src.rearrange("(p j) w -> p j w", j=PACK))
            return t

        def load_row_vector(name, src):
            t = tile(name, [P, PACK], F32)
            nc.sync.dma_start(out=t[:], in_=src.rearrange("(p r) o -> p (r o)", r=PACK))
            return t

        nc.sync.dma_start(offs_t[:], offs)
        nc.sync.dma_start(out=rows[0:8, :], in_=fade.rearrange("o (c n) -> (o c) n", n=P))
        key_words = load_words("key_words", keys_words)
        load_scale_rows(key_bytes, keys_scales)
        query_raw = load_k_first("query_raw", query)
        age_t = tile("age_t", [P, T], F32)
        nc.sync.dma_start(out=age_t[:], in_=age)
        val_words = load_words("val_words", vals_words)
        rate_t = load_row_vector("rate_t", rate)
        size_t = tile("size_t", [P, 2], F32)
        nc.sync.dma_start(out=size_t[:], in_=size.rearrange("o (n c) -> (o n) c", c=2))
        qs_t = load_row_vector("qs_t", qs)
        reserve_t = load_row_vector("reserve_t", reserve)
        gout_raw = load_k_first("gout_raw", gout)
        load_scale_rows(val_bytes, vals_scales)
        qrows_raw = load_k_first("qrows_raw", qrows)
        old_first = tile("old_first", [P, U], F32)
        nc.sync.dma_start(out=old_first[:], in_=old[0:P, :])
        old_half = []
        for h in range(2):
            t = tile("old_half%d" % h, [P, 4 - NG, 512], F32)
            nc.sync.dma_start(out=t[:], in_=old[P * NG :, 512 * h : 512 * (h + 1)].rearrange("(k m) u -> m k u", m=P))
            old_half.append(t)
        nc.sync.dma_start(offs4_t[:], offs4)
        placed = []
        for k in range(4):
            t = tile("placed%d" % k, [P, U], F32)
            (nc.vector if k < 2 else nc.gpsimd).memset(t[:], 0.0)
            placed.append(t)

        def gather(name, window, dtype):
            t = tile(name, [P, I], dtype)
            nc.vector.tensor_copy(t[:], window[:].indirect(offs_t[:]))
            return t

        def planes(name, width, tag=None):
            return tile(name + "_codes", [P, width], U32, tag=tag), tile(name + "_scales", [P, width], U8)

        def quantise(operand, cols, grouped):
            codes, scales = operand
            nc.vector.quantize_mx(out=codes[:, cols].bitcast(FP8X4), scales=scales[:, cols], in_=grouped[:])

        def product(acc, stationary, s_cols, moving, m_cols, moving_dtype):
            nc.tensor.matmul_mx(
                out=acc,
                lhsT=stationary[0][:, s_cols].bitcast(FP8X4),
                lhsT_scale=stationary[1][:, s_cols],
                rhs=moving[0][:, m_cols].bitcast(moving_dtype),
                rhs_scale=moving[1][:, m_cols],
                start=True,
                stop=True,
            )

        def deal(name, raw, h, on_vector):
            grouped = tile("%s_bf%d" % (name, h), [P, 2 * P * PACK], BF16)
            dst = grouped[:].rearrange("p (r s j) -> p s j r", r=2, j=PACK)
            src = raw[:].rearrange("p j (s r) -> p s j r", r=PACK)[:, :, :, 2 * h : 2 * h + 2]
            if h in on_vector:
                nc.vector.tensor_copy(out=dst, in_=src)
            else:
                nc.scalar.activation(dst, src, ACT.Copy)
            return grouped

        def listed_product(name, grouped, words, scale_bytes, tags, codes_tag=None):
            operand = planes(name, Q, codes_tag)
            banks = []
            for h in range(2):
                quantise(operand, slice(2 * P * h, 2 * P * (h + 1)), grouped[h])
                acc = bank("%s_acc%d" % (name, h), tags[h], [P, 2, I])
                for rr in range(2):
                    r = 2 * h + rr
                    product(acc[:, rr, :], operand, slice(P * r, P * (r + 1)), (words, scale_bytes), slice(0, I), FP4X4)
                banks.append(acc)
            return banks

        key_g = gather("key_g", key_words, U16)
        key_sg = gather("key_sg", key_bytes, U8)
        turned = bank("turned", "x1", [P, P])
        nc.tensor.transpose(turned[:], rows[:], ident[:])
        cols = tile("cols", [P, 8], F32)
        nc.scalar.copy(cols[:], turned[:, 0:8])

        fade_all = tile("fade_all", [P, U], F32)
        for h in range(2):
            spread = bank("spread%d" % h, "x%d" % h, [P, 4, P])
            for cc in range(4):
                c = 4 * h + cc
                nc.tensor.transpose(spread[:, cc, :], cols[:, c : c + 1].to_broadcast([P, P]), ident[:])
            nc.scalar.copy(fade_all[:, 512 * h : 512 * (h + 1)], spread[:].rearrange("p c n -> p (c n)"))

        val_g = gather("val_g", val_words, U16)
        query_bf = [deal("query", query_raw, h, [0]) for h in range(2)]
        score = listed_product("query", query_bf, key_g, key_sg, ["a0", "a1"])
        age_g = gather("age_g", age_t, F32)

        neg_t = tile("neg_t", [P, PACK, I], F32)
        p_t = tile("p_t", [P, PACK, I], F32)
        row_sum = tile("row_sum", [P, PACK], F32)
        for r in range(PACK):
            nc.vector.scalar_tensor_tensor(
                out=neg_t[:, r, :], in0=age_g[:], scalar=rate_t[:, r : r + 1], in1=score[r // 2][:, r % 2, :],
                op0=ALU.mult, op1=ALU.subtract,
            )
            nc.scalar.activation(p_t[:, r, :], neg_t[:, r, :], ACT.Exp, scale=-1.0, accum_out=row_sum[:, r : r + 1])


        size_all = bank("size_all", "sz", [P, 2, P])
        for c in range(2):
            nc.tensor.transpose(size_all[:, c, :], size_t[:, c : c + 1].to_broadcast([P, P]), ident[:])

        z = tile("z", [P, PACK], F32)
        z_inv = tile("z_inv", [P, PACK], F32)
        nc.vector.tensor_tensor(z[:], row_sum[:], reserve_t[:], ALU.add)
        nc.vector.reciprocal(z_inv[:], z[:])

        gout_bf = [deal("gout", gout_raw, h, []) for h in range(2)]
        val_sg = gather("val_sg", val_bytes, U8)
        c0 = listed_product("gout", gout_bf, val_g, val_sg, ["c0", "c1"], codes_tag="val_bytes")

        p_size = tile("p_size", [P, PACK, I], F32)
        for r in range(PACK):
            nc.vector.scalar_tensor_tensor(
                out=p_size[:, r, :].rearrange("p (n c) -> p n c", c=2),
                in0=p_t[:, r, :].rearrange("p (n c) -> p n c", c=2),
                scalar=qs_t[:, r : r + 1],
                in1=size_all[:].rearrange("p c n -> p n c"),
                op0=ALU.mult, op1=ALU.mult,
            )

        direct = tile("direct", [P, PACK, I], F32)
        direct_sum = tile("direct_sum", [P, PACK], F32)
        through_z = tile("through_z", [P, PACK, I], F32)
        for r in range(PACK):
            nc.vector.scalar_tensor_tensor(
                out=direct[:, r, :], in0=c0[r // 2][:, r % 2, :], scalar=z_inv[:, r : r + 1], in1=p_size[:, r, :],
                op0=ALU.mult, op1=ALU.mult, accum_out=direct_sum[:, r : r + 1],
            )
        for r in range(PACK):
            nc.vector.tensor_scalar(
                through_z[:, r, :], p_t[:, r, :], direct_sum[:, r : r + 1], z_inv[:, r : r + 1], ALU.mult, ALU.mult
            )

        qrows_q = planes("qrows", D)
        for h in range(2):
            grouped = tile("qrows_bf%d" % h, [P, 2 * P * PACK], BF16)
            nc.scalar.copy(
                grouped[:].rearrange("p (c i j) -> p c j i", i=4, j=PACK),
                qrows_raw[:, :, 2 * P * h : 2 * P * (h + 1)].rearrange("p j (c i) -> p c j i", i=4),
            )
            quantise(qrows_q, slice(2 * P * h, 2 * P * (h + 1)), grouped)

        gs_q = planes("gs", I)
        for b in range(2):
            slots = slice(P * b, P * (b + 1))
            gs_bf = tile("gs_bf%d" % b, [P, P * PACK], BF16, tag="qrows_bf0")
            nc.vector.tensor_tensor(
                gs_bf[:].rearrange("p (c i r) -> p c r i", i=4, r=PACK),
                direct[:, :, slots].rearrange("p r (c i) -> p c r i", i=4),
                through_z[:, :, slots].rearrange("p r (c i) -> p c r i", i=4),
                ALU.subtract,
            )
            quantise(gs_q, slots, gs_bf)

        faded_t = []

        def fade_turned(c):
            stage = bank("stage%d" % c, ["x0", "x1", "y0", "sz", "x0", "x1", "x1", "x1"][c], [P, 4 - NG, P])
            for k in range(4 - NG):
                nc.tensor.transpose(stage[:, k, :], old_half[c // 4][:, k, P * (c % 4) : P * (c % 4 + 1)], ident[:])
            t = tile("faded_t%d" % c, [P, (4 - NG) * P], F32)
            nc.scalar.activation(t[:], stage[:].rearrange("p k m -> p (k m)"), ACT.Copy, scale=cols[:, c : c + 1])
            faded_t.append(t)

        gk = {}

        def key_gradient(tag, pieces):
            acc = bank("gk_acc%d_%d" % pieces[0][:2], tag, [P, 512])
            places = []
            for k, lo, hi in pieces:
                start = sum(b - a for a, b in places)
                places.append((start, start + hi - lo))
                product(acc[:, start : start + hi - lo], qrows_q, slice(P * k, P * (k + 1)), gs_q, slice(lo, hi), FP8X4)
            for (k, lo, hi), (a, b) in zip(pieces, places):
                gk[k, lo] = tile("gk%d_%d" % (k, lo), [P, hi - lo], F32)
                nc.scalar.copy(gk[k, lo][:], acc[:, a:b])

        for c in range(6):
            fade_turned(c)
        key_gradient("x0", [(0, 0, P), (1, 0, P)])
        key_gradient("x1", [(0, P, I), (1, P, I)])
        key_gradient("x0", [(2, 0, I), (3, 0, I)])
        fade_turned(6)
        fade_turned(7)

        for k, lo, hi in [(0, 0, P), (1, 0, P), (0, P, I), (1, P, I), (2, 0, I), (3, 0, I)]:
            nc.vector.tensor_copy(placed[k][:].indirect(offs4_t[:, lo // 16 : hi // 16]), gk[k, lo][:])

        def finish(engine, queue, k, h, faded, res):
            half = slice(512 * h, 512 * (h + 1))
            engine.tensor_tensor(res, faded, placed[k][:, half], ALU.add)
            queue.dma_start(out=out[P * k : P * (k + 1), half], in_=res)

        def turned_back(k, h, tag):
            faded = bank("faded%d_%d" % (k, h), tag, [P, 4, P])
            for cc in range(4):
                nc.tensor.transpose(faded[:, cc, :], faded_t[4 * h + cc][:, P * (k - 1) : P * k], ident[:])
            return faded[:].rearrange("p c n -> p (c n)")

        faded_first = []
        for h in range(2):
            half = slice(512 * h, 512 * (h + 1))
            t = tile("faded_first%d" % h, [P, 512], F32, tag=["gout_bf1", "qrows_bf0"][h])
            nc.gpsimd.tensor_tensor(t[:], old_first[:, half], fade_all[:, half], ALU.mult)
            faded_first.append(t)
        for h in range(2):
            res = tile("res0_%d" % h, [P, 512], F32)
            finish(nc.gpsimd, nc.sync, 0, h, faded_first[h][:], res[:])

        for h in range(2):
            moved = tile("moved%d" % h, [P, 512], F32)
            nc.scalar.copy(moved[:], turned_back(1, h, "x%d" % h))
            res = tile("res1_%d" % h, [P, 512], F32)
            finish(nc.gpsimd, [nc.sync, nc.scalar][h], 1, h, moved[:], res[:])

        res_last = tile("res_last", [P, 4, 512], F32, tag="moved0")
        for n, tag in enumerate(["a0", "a1", "c0", "c1"]):
            k, h = 2 + n // 2, n % 2
            finish(nc.vector, nc.sync, k, h, turned_back(k, h, tag), res_last[:, n, :])
